import numpy as np
import ml_dtypes


def mxq(x, axis, fmt="e4m3"):
    dtype, down = {"e4m3": (ml_dtypes.float8_e4m3fn, 7), "e5m2": (ml_dtypes.float8_e5m2, 14)}[fmt]
    v = np.moveaxis(np.asarray(x, np.float32).astype(ml_dtypes.bfloat16).astype(np.float64), axis, -1)
    blocks = v.reshape(v.shape[:-1] + (-1, 32))
    amax = np.abs(blocks).max(-1, keepdims=True)
    byte = np.maximum(np.where(amax > 0, np.frexp(amax)[1] - 1 + 127, 0) - down, 1)
    scale = np.exp2(byte - 127.0)
    codes = (blocks / scale).astype(np.float32).astype(dtype).astype(np.float64)
    return np.moveaxis((codes * scale).reshape(v.shape), -1, axis)


WIDE = False


def mx_kscale(k):
    if not WIDE:
        return np.ones(k)
    levels = np.array([10, -10, 5, -5, 0])
    if k % 512:
        return np.exp2(np.random.permutation(np.resize(levels, k // 32))).repeat(32)
    a = np.empty((k // 512, 16))
    for p in range(k // 512):
        a[p, :8] = np.random.permutation(np.resize(levels, 8))
        for g in range(8):
            far = levels[np.abs(levels - a[p, g]) >= 10]
            a[p, g + 8] = far[np.random.randint(len(far))]
    return np.exp2(a.ravel()).repeat(32)


def f64(x):
    return np.asarray(x).astype(np.float64)


def striped(idx):
    return np.tile(idx.reshape(-1, 16).T, (8, 1)).astype(np.uint16)


def unstriped(offs):
    return offs[:16].T.reshape(-1).astype(np.int64)


def striped8(idx):
    return np.concatenate([x.reshape(-1, 16).T for x in idx]).astype(np.uint16)


def runs(offs, k):
    lists = np.stack([offs[16 * r : 16 * r + 16].T.reshape(-1) for r in range(8)]).astype(np.int64)
    return lists[np.arange(k) % 512 // 64]


def pack_weight(w):
    k, n = w.shape
    w = f64(np.asarray(w, np.float32).astype(ml_dtypes.bfloat16)).reshape(k // 32, 32, n)
    amax = np.abs(w).max(1)
    byte = np.clip(np.where(amax > 0, np.frexp(amax)[1] - 1 + 127 - 7, 1), 1, 254)
    scaled = (w * np.exp2(127.0 - byte)[:, None, :]).reshape(k, n).astype(np.float32)
    words = np.ascontiguousarray(scaled.reshape(k // 512, 128, 4, n).transpose(0, 1, 3, 2)).astype(ml_dtypes.float8_e4m3fn).view(np.uint8)
    return words, np.ascontiguousarray(byte.astype(np.uint8).reshape(k // 512, 16, n))


def unpack_weight(words, scales):
    g, p, n, _ = words.shape
    vals = np.ascontiguousarray(words).view(ml_dtypes.float8_e4m3fn).astype(np.float64) * np.repeat(np.exp2(scales.astype(np.float64) - 127.0), 8, axis=1)[..., None]
    return vals.transpose(0, 1, 3, 2).reshape(g * 512, n)


def sigmoid(v):
    return 1.0 / (1.0 + np.exp(-np.maximum(v, -700.0)))


K, T, S, N, H, W = 512, 2048, 512, 512, 512, 2048


def setup_inputs():
    n = np.random.standard_normal
    s = mx_kscale(K)[:, None]
    u = mx_kscale(H)
    packed_xT = pack_weight(n((K, T)) * s)
    return {
        "x_words": packed_xT[0],
        "x_scales": packed_xT[1],
        "w1": (n((K, H)) / np.sqrt(K) / s).astype(np.float32),
        "gn": (np.random.uniform(0.5, 1.5, (H, 1)) * u[:, None]).astype(np.float32),
        "w2": (n((H, N)) / np.sqrt(2 * H) / u[:, None]).astype(np.float32),
        "w3": (n((K, N)) / np.sqrt(2 * K) / s).astype(np.float32),
        "offs": striped(np.random.permutation(T)[:S]),
        "n1": striped8(np.stack([np.random.permutation(S) for _ in range(8)])),
        "n2": striped8(np.stack([np.random.permutation(S) for _ in range(8)])),
        "two": striped(np.random.permutation(T)[:S]),
        "n3": striped(np.random.randint(0, S, W)),
    }


def reference(x_words, x_scales, w1, gn, w2, w3, offs, n1, n2, two, n3):
    xq = unpack_weight(x_words, x_scales)[:, unstriped(offs)]
    y = mxq(f64(w1), 0, "e4m3").T @ xq
    z = f64(gn) * (np.maximum(y * (sigmoid(y[np.arange(H)[:, None], runs(n1, H)])), y[np.arange(H)[:, None], runs(n2, H)]))
    x_two = unpack_weight(x_words, x_scales)[:, unstriped(two)]
    h = mxq(f64(w2), 0, "e4m3").T @ mxq(z, 0, "e4m3") + mxq(f64(w3), 0, "e4m3").T @ x_two
    ex = np.exp(h)
    mb = ex[:, unstriped(n3)]
    ms = mb.reshape(N, S, 4).sum(axis=2)
    return np.log(ms + ex) - h

@@ -1,0 +1,258 @@
+from contextlib import ExitStack
+
+import concourse.mybir as mybir
+
+K, T, S, N, H, W = 512, 2048, 512, 512, 512, 2048
+FLOPS = 2 * S * (K * H + H * N + K * N)
+
+F32 = mybir.dt.float32
+BF16 = mybir.dt.bfloat16
+I32 = mybir.dt.int32
+U32 = mybir.dt.uint32
+U16 = mybir.dt.uint16
+U8 = mybir.dt.uint8
+FP8X4 = mybir.dt.float8_e4m3fn_x4
+ACT = mybir.ActivationFunctionType
+ALU = mybir.AluOpType
+
+P = 128
+PACK = 4
+STRIPE = 16
+HALF = S // 2
+MEMBERS = W // S
+SPARE = 32
+PIECE = 512
+Z_CHUNKS = ((0, 256), (256, 512))
+VECTOR_PIECES = ((0, 1), (0,), (0,), (0, 1))
+Y_ON_VECTOR = (0, 1)
+
+
+def tile_picked_mixingmaxglse_none_p_kernel(
+    tc, x_words, x_scales, w1, gn, w2, w3, offs, n1, n2, two, n3, out
+):
+    nc = tc.nc
+    with ExitStack() as ctx:
+        keep = ctx.enter_context(tc.tile_pool(name="keep", bufs=1))
+        psum = ctx.enter_context(tc.psum_pool(name="psum", bufs=1))
+
+        def sb(name, shape, dtype):
+            return keep.tile(shape, dtype, name=name, align_bytes=64)
+
+        offs_t = sb("offs_t", [P, S // STRIPE], U16)
+        two_t = sb("two_t", [P, S // STRIPE], U16)
+        n1_t = sb("n1_t", [P, S // STRIPE], U16)
+        n2_t = sb("n2_t", [P, S // STRIPE], U16)
+        n3_t = sb("n3_t", [P, W // STRIPE], U16)
+        xw = sb("xw", [P, T], U32)
+        xs = sb("xs", [P, T], U8)
+        w1_raw = sb("w1_raw", [P, PACK, H], F32)
+        w2_raw = sb("w2_raw", [P, PACK, N], F32)
+        w3_raw = sb("w3_raw", [P, PACK, N], F32)
+        gain = sb("gain", [P, PACK], F32)
+        ex = [sb("ex%d" % m, [P, S + SPARE], F32) for m in range(N // P)]
+
+        nc.gpsimd.memset(xs[:].bitcast(I32), 0)
+        for m in range(N // P):
+            nc.gpsimd.memset(ex[m][:, S:], 0.0)
+
+        nc.sync.dma_start(offs_t[:], offs)
+        nc.sync.dma_start(out=w1_raw[:], in_=w1.rearrange("(p j) c -> p j c", j=PACK))
+        for q in range(4):
+            nc.scalar.dma_start(
+                out=xs[32 * q : 32 * q + 4, :].bitcast(I32),
+                in_=x_scales[0, 4 * q : 4 * q + 4, :].bitcast(I32),
+            )
+        nc.sync.dma_start(out=xw[:].bitcast(I32), in_=x_words[0].rearrange("p n t -> p (n t)").bitcast(I32))
+        nc.sync.dma_start(two_t[:], two)
+        nc.sync.dma_start(out=w3_raw[:], in_=w3.rearrange("(p j) c -> p j c", j=PACK))
+        nc.sync.dma_start(n1_t[:], n1)
+        nc.sync.dma_start(n2_t[:], n2)
+        nc.sync.dma_start(out=gain[:], in_=gn.rearrange("(p t) o -> p (t o)", t=PACK))
+        nc.sync.dma_start(out=w2_raw[:], in_=w2.rearrange("(p j) c -> p j c", j=PACK))
+        nc.sync.dma_start(n3_t[:], n3)
+
+        def cols(lst, a, b):
+            return lst[:, a // STRIPE : b // STRIPE]
+
+        w1_codes = [sb("w1_codes%d" % u, [P, 2 * P], U32) for u in range(2)]
+        w1_scales = [sb("w1_scales%d" % u, [P, 2 * P], U8) for u in range(2)]
+        w1_bf = [sb("w1_bf%d" % u, [P, 2, P, PACK], BF16) for u in range(2)]
+        for u in range(2):
+            nc.scalar.copy(
+                out=w1_bf[u][:].rearrange("p t m j -> p m j t"),
+                in_=w1_raw[:].rearrange("p j (m t) -> p m j t", t=PACK)[:, :, :, 2 * u : 2 * u + 2],
+            )
+
+        xa_s = sb("xa_s", [P, S], U8)
+        xb_s = sb("xb_s", [P, S], U8)
+        xa_w = [sb("xa_w%d" % c, [P, HALF], U32) for c in range(2)]
+        xb_w = sb("xb_w", [P, S], U32)
+        nc.vector.tensor_copy(out=xa_s[:], in_=xs[:].indirect(offs_t[:]))
+        nc.vector.tensor_copy(out=xb_s[:], in_=xs[:].indirect(two_t[:]))
+
+        def quantize(codes, scales, values):
+            nc.vector.quantize_mx(out=codes.bitcast(FP8X4), scales=scales, in_=values)
+
+        quantize(w1_codes[0][:], w1_scales[0][:], w1_bf[0][:].rearrange("p t m j -> p (t m j)"))
+        for c in range(2):
+            nc.vector.tensor_copy(out=xa_w[c][:], in_=xw[:].indirect(cols(offs_t, c * HALF, (c + 1) * HALF)))
+        quantize(w1_codes[1][:], w1_scales[1][:], w1_bf[1][:].rearrange("p t m j -> p (t m j)"))
+
+        y_ps = [psum.tile([P, S], F32, name="y_ps%d" % t, tag="bank%d" % t) for t in range(PACK)]
+        for pair in range(2):
+            for c in range(2):
+                for t in (2 * pair, 2 * pair + 1):
+                    mc = slice((t % 2) * P, (t % 2 + 1) * P)
+                    nc.tensor.matmul_mx(
+                        out=y_ps[t][:, c * HALF : (c + 1) * HALF],
+                        lhsT=w1_codes[pair][:, mc].bitcast(FP8X4),
+                        lhsT_scale=w1_scales[pair][:, mc],
+                        rhs=xa_w[c][:].bitcast(FP8X4),
+                        rhs_scale=xa_s[:, c * HALF : (c + 1) * HALF],
+                        start=True,
+                        stop=True,
+                    )
+
+        y = [sb("y%d" % t, [P, S], F32) for t in range(PACK)]
+        gate = [sb("gate%d" % c, [P, PACK, b - a], F32) for c, (a, b) in enumerate(Z_CHUNKS)]
+        other = [sb("other%d" % c, [P, PACK, b - a], F32) for c, (a, b) in enumerate(Z_CHUNKS)]
+        gated = [sb("gated%d" % c, [P, PACK, b - a], F32) for c, (a, b) in enumerate(Z_CHUNKS)]
+        larger = [sb("larger%d" % c, [P, PACK, b - a], F32) for c, (a, b) in enumerate(Z_CHUNKS)]
+        z_bf = [sb("z_bf%d" % c, [P, b - a, PACK], BF16) for c, (a, b) in enumerate(Z_CHUNKS)]
+        z_codes = [sb("z_codes%d" % c, [P, b - a], U32) for c, (a, b) in enumerate(Z_CHUNKS)]
+        z_scales = [sb("z_scales%d" % c, [P, b - a], U8) for c, (a, b) in enumerate(Z_CHUNKS)]
+
+        def copy_y(t):
+            if t in Y_ON_VECTOR:
+                nc.vector.tensor_copy(out=y[t][:], in_=y_ps[t][:])
+            else:
+                nc.scalar.copy(out=y[t][:], in_=y_ps[t][:])
+
+        def gather_gate(c, t):
+            a, b = Z_CHUNKS[c]
+            nc.scalar.activation(out=gate[c][:, t, :], in_=y[t][:].indirect(cols(n1_t, a, b)), func=ACT.Sigmoid)
+
+        def gather_other(c, t):
+            a, b = Z_CHUNKS[c]
+            nc.scalar.activation(out=other[c][:, t, :], in_=y[t][:].indirect(cols(n2_t, a, b)), func=ACT.Copy)
+
+        def apply_gate(c, t):
+            a, b = Z_CHUNKS[c]
+            nc.vector.tensor_tensor(out=gated[c][:, t, :], in0=gate[c][:, t, :], in1=y[t][:, a:b], op=ALU.mult)
+
+        def take_larger(c, t):
+            nc.vector.tensor_tensor(out=larger[c][:, t, :], in0=gated[c][:, t, :], in1=other[c][:, t, :], op=ALU.max)
+
+        def make_z(c):
+            a, b = Z_CHUNKS[c]
+            nc.vector.tensor_tensor(
+                out=z_bf[c][:].rearrange("p (g i) t -> p g t i", i=4),
+                in0=larger[c][:].rearrange("p t (g i) -> p g t i", i=4),
+                in1=gain[:].unsqueeze(1).unsqueeze(3).to_broadcast([P, (b - a) // 4, PACK, 4]),
+                op=ALU.mult,
+            )
+            quantize(z_codes[c][:], z_scales[c][:], z_bf[c][:].rearrange("p j t -> p (j t)"))
+
+        def prepare_weight(name, raw):
+            bf = sb(name + "_bf", [P, N, PACK], BF16)
+            codes = sb(name + "_codes", [P, N], U32)
+            scales = sb(name + "_scales", [P, N], U8)
+            nc.vector.tensor_copy(
+                out=bf[:].rearrange("p (g i) j -> p g j i", i=4),
+                in_=raw[:].rearrange("p j (g i) -> p g j i", i=4),
+            )
+            return bf, codes, scales
+
+        for t in Y_ON_VECTOR:
+            copy_y(t)
+        nc.vector.tensor_copy(out=xb_w[:], in_=xw[:].indirect(two_t[:]))
+        w3_bf, w3_codes, w3_scales = prepare_weight("w3", w3_raw)
+        w2_bf, w2_codes, w2_scales = prepare_weight("w2", w2_raw)
+        quantize(w3_codes[:], w3_scales[:], w3_bf[:].rearrange("p n j -> p (n j)"))
+        quantize(w2_codes[:], w2_scales[:], w2_bf[:].rearrange("p n j -> p (n j)"))
+        for t in range(PACK):
+            if t not in Y_ON_VECTOR:
+                copy_y(t)
+            gather_gate(0, t)
+            gather_other(0, t)
+            apply_gate(0, t)
+            take_larger(0, t)
+        make_z(0)
+        for c in range(1, len(Z_CHUNKS)):
+            for t in range(PACK):
+                gather_gate(c, t)
+                apply_gate(c, t)
+            for t in range(PACK):
+                gather_other(c, t)
+                take_larger(c, t)
+            make_z(c)
+
+        h_ps = [
+            [psum.tile([P, HALF], F32, name="h_ps%d_%d" % (m, hf), tag="bank%d" % (m + 4 * (1 - hf))) for hf in range(2)]
+            for m in range(N // P)
+        ]
+        for hf in range(2):
+            for m in range(N // P):
+                mc = slice(m * P, (m + 1) * P)
+                nc.tensor.matmul_mx(
+                    out=h_ps[m][hf][:],
+                    lhsT=w3_codes[:, mc].bitcast(FP8X4),
+                    lhsT_scale=w3_scales[:, mc],
+                    rhs=xb_w[:, hf * HALF : (hf + 1) * HALF].bitcast(FP8X4),
+                    rhs_scale=xb_s[:, hf * HALF : (hf + 1) * HALF],
+                    start=True,
+                    stop=False,
+                )
+        for c, (a, b) in enumerate(Z_CHUNKS):
+            hf = a // HALF
+            for m in range(N // P):
+                mc = slice(m * P, (m + 1) * P)
+                nc.tensor.matmul_mx(
+                    out=h_ps[m][hf][:, a - hf * HALF : b - hf * HALF],
+                    lhsT=w2_codes[:, mc].bitcast(FP8X4),
+                    lhsT_scale=w2_scales[:, mc],
+                    rhs=z_codes[c][:].bitcast(FP8X4),
+                    rhs_scale=z_scales[c][:],
+                    start=False,
+                    stop=(b == (hf + 1) * HALF),
+                )
+        for hf in range(2):
+            for m in range(N // P):
+                nc.scalar.activation(out=ex[m][:, hf * HALF : (hf + 1) * HALF], in_=h_ps[m][hf][:], func=ACT.Exp)
+
+        members = [sb("members%d" % m, [P, S, MEMBERS], F32) for m in range(N // P)]
+        pairs = [sb("pairs%d" % m, [P, S, 2], F32) for m in range(N // P)]
+        sums = [sb("sums%d" % m, [P, S], F32) for m in range(N // P)]
+        total = [sb("total%d" % m, [P, S], F32) for m in range(N // P)]
+        logs = [sb("logs%d" % m, [P, S], F32) for m in range(N // P)]
+        res = [sb("res%d" % m, [P, S], F32) for m in range(N // P)]
+
+        def gather_members(m):
+            flat = members[m][:].rearrange("p j t -> p (j t)")
+            for i in range(W // PIECE):
+                src = ex[m][:].indirect(cols(n3_t, i * PIECE, (i + 1) * PIECE))
+                dst = flat[:, i * PIECE : (i + 1) * PIECE]
+                if i in VECTOR_PIECES[m]:
+                    nc.vector.tensor_copy(out=dst, in_=src)
+                else:
+                    nc.scalar.activation(out=dst, in_=src, func=ACT.Copy)
+
+        def add_members(m, a, b):
+            nc.vector.tensor_tensor(out=pairs[m][:, a:b, :], in0=members[m][:, a:b, 0:2], in1=members[m][:, a:b, 2:4], op=ALU.add)
+            nc.vector.tensor_tensor(out=sums[m][:, a:b], in0=pairs[m][:, a:b, 0], in1=pairs[m][:, a:b, 1], op=ALU.add)
+            nc.vector.tensor_tensor(out=total[m][:, a:b], in0=sums[m][:, a:b], in1=ex[m][:, a:b], op=ALU.add)
+
+        def finish(m, hf):
+            a, b = hf * HALF, (hf + 1) * HALF
+            nc.scalar.activation(out=logs[m][:, a:b], in_=total[m][:, a:b], func=ACT.Ln)
+            nc.vector.tensor_tensor(out=res[m][:, a:b], in0=logs[m][:, a:b], in1=h_ps[m][hf][:], op=ALU.subtract)
+            nc.sync.dma_start(out=out[m * P : (m + 1) * P, a:b], in_=res[m][:, a:b])
+
+        gather_members(0)
+        for m in range(N // P):
+            if m + 1 < N // P:
+                gather_members(m + 1)
+            for hf in range(2):
+                add_members(m, hf * HALF, (hf + 1) * HALF)
+            for hf in range(2):
+                finish(m, hf)

@@ -1,6 +1,7 @@
 from contextlib import ExitStack
 
 import concourse.mybir as mybir
+from concourse.masks import make_identity
 
 K, T, S, N, H, W = 512, 2048, 512, 512, 512, 2048
 FLOPS = 2 * S * (K * H + H * N + K * N)
@@ -23,8 +24,8 @@ MEMBERS = W // S
 SPARE = 32
 PIECE = 512
 Z_CHUNKS = ((0, 256), (256, 512))
-VECTOR_PIECES = ((0, 1), (0,), (0,), (0, 1))
-Y_ON_VECTOR = (0, 1)
+TENSOR_TILES = (0, 1)
+Y_ON_VECTOR = (1, 2)
 
 
 def tile_picked_mixingmaxglse_none_p_kernel(
@@ -35,8 +36,8 @@ def tile_picked_mixingmaxglse_none_p_kernel(
         keep = ctx.enter_context(tc.tile_pool(name="keep", bufs=1))
         psum = ctx.enter_context(tc.psum_pool(name="psum", bufs=1))
 
-        def sb(name, shape, dtype):
-            return keep.tile(shape, dtype, name=name, align_bytes=64)
+        def sb(name, shape, dtype, tag=None):
+            return keep.tile(shape, dtype, name=name, tag=tag or name, align_bytes=64)
 
         offs_t = sb("offs_t", [P, S // STRIPE], U16)
         two_t = sb("two_t", [P, S // STRIPE], U16)
@@ -55,18 +56,24 @@ def tile_picked_mixingmaxglse_none_p_kernel(
         for m in range(N // P):
             nc.gpsimd.memset(ex[m][:, S:], 0.0)
 
+        ident = sb("ident", [P, P], F32)
+        make_identity(nc, ident[:])
+
+        warm = sb("warm", [P, 1], F32)
+        nc.scalar.activation(out=warm[:], in_=ex[0][:, S : S + 1], func=ACT.Sigmoid)
+
         nc.sync.dma_start(offs_t[:], offs)
-        nc.sync.dma_start(out=w1_raw[:], in_=w1.rearrange("(p j) c -> p j c", j=PACK))
+        nc.sync.dma_start(two_t[:], two)
         for q in range(4):
-            nc.scalar.dma_start(
+            nc.sync.dma_start(
                 out=xs[32 * q : 32 * q + 4, :].bitcast(I32),
                 in_=x_scales[0, 4 * q : 4 * q + 4, :].bitcast(I32),
             )
+        nc.sync.dma_start(out=w1_raw[:], in_=w1.rearrange("(p j) c -> p j c", j=PACK))
         nc.sync.dma_start(out=xw[:].bitcast(I32), in_=x_words[0].rearrange("p n t -> p (n t)").bitcast(I32))
-        nc.sync.dma_start(two_t[:], two)
-        nc.sync.dma_start(out=w3_raw[:], in_=w3.rearrange("(p j) c -> p j c", j=PACK))
         nc.sync.dma_start(n1_t[:], n1)
         nc.sync.dma_start(n2_t[:], n2)
+        nc.sync.dma_start(out=w3_raw[:], in_=w3.rearrange("(p j) c -> p j c", j=PACK))
         nc.sync.dma_start(out=gain[:], in_=gn.rearrange("(p t) o -> p (t o)", t=PACK))
         nc.sync.dma_start(out=w2_raw[:], in_=w2.rearrange("(p j) c -> p j c", j=PACK))
         nc.sync.dma_start(n3_t[:], n3)
@@ -77,11 +84,6 @@ def tile_picked_mixingmaxglse_none_p_kernel(
         w1_codes = [sb("w1_codes%d" % u, [P, 2 * P], U32) for u in range(2)]
         w1_scales = [sb("w1_scales%d" % u, [P, 2 * P], U8) for u in range(2)]
         w1_bf = [sb("w1_bf%d" % u, [P, 2, P, PACK], BF16) for u in range(2)]
-        for u in range(2):
-            nc.scalar.copy(
-                out=w1_bf[u][:].rearrange("p t m j -> p m j t"),
-                in_=w1_raw[:].rearrange("p j (m t) -> p m j t", t=PACK)[:, :, :, 2 * u : 2 * u + 2],
-            )
 
         xa_s = sb("xa_s", [P, S], U8)
         xb_s = sb("xb_s", [P, S], U8)
@@ -93,10 +95,17 @@ def tile_picked_mixingmaxglse_none_p_kernel(
         def quantize(codes, scales, values):
             nc.vector.quantize_mx(out=codes.bitcast(FP8X4), scales=scales, in_=values)
 
-        quantize(w1_codes[0][:], w1_scales[0][:], w1_bf[0][:].rearrange("p t m j -> p (t m j)"))
+        for u, cast in enumerate((nc.scalar.copy, nc.vector.tensor_copy)):
+            cast(
+                out=w1_bf[u][:].rearrange("p t m j -> p m j t"),
+                in_=w1_raw[:].rearrange("p j (m t) -> p m j t", t=PACK)[:, :, :, 2 * u : 2 * u + 2],
+            )
+        for u in range(2):
+            quantize(w1_codes[u][:], w1_scales[u][:], w1_bf[u][:].rearrange("p t m j -> p (t m j)"))
+
         for c in range(2):
             nc.vector.tensor_copy(out=xa_w[c][:], in_=xw[:].indirect(cols(offs_t, c * HALF, (c + 1) * HALF)))
-        quantize(w1_codes[1][:], w1_scales[1][:], w1_bf[1][:].rearrange("p t m j -> p (t m j)"))
+        nc.vector.tensor_copy(out=xb_w[:], in_=xw[:].indirect(two_t[:]))
 
         y_ps = [psum.tile([P, S], F32, name="y_ps%d" % t, tag="bank%d" % t) for t in range(PACK)]
         for pair in range(2):
@@ -116,7 +125,7 @@ def tile_picked_mixingmaxglse_none_p_kernel(
         y = [sb("y%d" % t, [P, S], F32) for t in range(PACK)]
         gate = [sb("gate%d" % c, [P, PACK, b - a], F32) for c, (a, b) in enumerate(Z_CHUNKS)]
         other = [sb("other%d" % c, [P, PACK, b - a], F32) for c, (a, b) in enumerate(Z_CHUNKS)]
-        gated = [sb("gated%d" % c, [P, PACK, b - a], F32) for c, (a, b) in enumerate(Z_CHUNKS)]
+        gated = [sb("gated%d" % c, [P, PACK, b - a], F32, tag="w2_raw") for c, (a, b) in enumerate(Z_CHUNKS)]
         larger = [sb("larger%d" % c, [P, PACK, b - a], F32) for c, (a, b) in enumerate(Z_CHUNKS)]
         z_bf = [sb("z_bf%d" % c, [P, b - a, PACK], BF16) for c, (a, b) in enumerate(Z_CHUNKS)]
         z_codes = [sb("z_codes%d" % c, [P, b - a], U32) for c, (a, b) in enumerate(Z_CHUNKS)]
@@ -165,7 +174,6 @@ def tile_picked_mixingmaxglse_none_p_kernel(
 
         for t in Y_ON_VECTOR:
             copy_y(t)
-        nc.vector.tensor_copy(out=xb_w[:], in_=xw[:].indirect(two_t[:]))
         w3_bf, w3_codes, w3_scales = prepare_weight("w3", w3_raw)
         w2_bf, w2_codes, w2_scales = prepare_weight("w2", w2_raw)
         quantize(w3_codes[:], w3_scales[:], w3_bf[:].rearrange("p n j -> p (n j)"))
@@ -216,6 +224,13 @@ def tile_picked_mixingmaxglse_none_p_kernel(
                     start=False,
                     stop=(b == (hf + 1) * HALF),
                 )
+        h_sb = {m: sb("h_sb%d" % m, [P, S], F32) for m in TENSOR_TILES}
+
+        def copy_h(hf):
+            for m in TENSOR_TILES:
+                nc.vector.tensor_copy(out=h_sb[m][:, hf * HALF : (hf + 1) * HALF], in_=h_ps[m][hf][:])
+
+        copy_h(0)
         for hf in range(2):
             for m in range(N // P):
                 nc.scalar.activation(out=ex[m][:, hf * HALF : (hf + 1) * HALF], in_=h_ps[m][hf][:], func=ACT.Exp)
@@ -226,33 +241,73 @@ def tile_picked_mixingmaxglse_none_p_kernel(
         total = [sb("total%d" % m, [P, S], F32) for m in range(N // P)]
         logs = [sb("logs%d" % m, [P, S], F32) for m in range(N // P)]
         res = [sb("res%d" % m, [P, S], F32) for m in range(N // P)]
+        turned = {m: psum.tile([P, S], F32, name="turned%d" % m, tag="bank%d" % (m + 4)) for m in TENSOR_TILES}
+        back = {m: psum.tile([P, S], F32, name="back%d" % m, tag="bank%d" % m) for m in TENSOR_TILES}
 
-        def gather_members(m):
-            flat = members[m][:].rearrange("p j t -> p (j t)")
-            for i in range(W // PIECE):
-                src = ex[m][:].indirect(cols(n3_t, i * PIECE, (i + 1) * PIECE))
-                dst = flat[:, i * PIECE : (i + 1) * PIECE]
-                if i in VECTOR_PIECES[m]:
-                    nc.vector.tensor_copy(out=dst, in_=src)
-                else:
-                    nc.scalar.activation(out=dst, in_=src, func=ACT.Copy)
+        def gather_members(engine, m, a, b):
+            src = ex[m][:].indirect(cols(n3_t, a * MEMBERS, b * MEMBERS))
+            dst = members[m][:, a:b, :].rearrange("p j t -> p (j t)")
+            if engine == "vector":
+                nc.vector.tensor_copy(out=dst, in_=src)
+            else:
+                nc.scalar.activation(out=dst, in_=src, func=ACT.Copy)
 
-        def add_members(m, a, b):
-            nc.vector.tensor_tensor(out=pairs[m][:, a:b, :], in0=members[m][:, a:b, 0:2], in1=members[m][:, a:b, 2:4], op=ALU.add)
-            nc.vector.tensor_tensor(out=sums[m][:, a:b], in0=pairs[m][:, a:b, 0], in1=pairs[m][:, a:b, 1], op=ALU.add)
-            nc.vector.tensor_tensor(out=total[m][:, a:b], in0=sums[m][:, a:b], in1=ex[m][:, a:b], op=ALU.add)
+        def add_turned(m, blk):
+            js = slice(blk * P, (blk + 1) * P)
+            terms = [members[m][:, js, t] for t in range(MEMBERS)] + [ex[m][:, js]]
+            for i, term in enumerate(terms):
+                nc.tensor.matmul(out=turned[m][:, js], lhsT=term, rhs=ident[:], is_transpose=True, start=(i == 0), stop=(i == MEMBERS))
 
-        def finish(m, hf):
-            a, b = hf * HALF, (hf + 1) * HALF
+        def log_turned(m):
+            nc.scalar.activation(out=logs[m][:], in_=turned[m][:], func=ACT.Ln)
+            for blk in range(S // P):
+                js = slice(blk * P, (blk + 1) * P)
+                nc.tensor.transpose(back[m][:, js], logs[m][:, js], ident[:])
+
+        def finish_turned(m):
+            nc.vector.tensor_tensor(out=res[m][:], in0=back[m][:], in1=h_sb[m][:], op=ALU.subtract)
+            nc.sync.dma_start(out=out[m * P : (m + 1) * P, :], in_=res[m][:])
+
+        def add_members(m):
+            halves = [slice(hf * HALF, (hf + 1) * HALF) for hf in range(2)]
+            for js in halves:
+                nc.vector.tensor_tensor(out=pairs[m][:, js, :], in0=members[m][:, js, 0:2], in1=members[m][:, js, 2:4], op=ALU.add)
+            for js in halves:
+                nc.vector.tensor_tensor(out=sums[m][:, js], in0=pairs[m][:, js, 0], in1=pairs[m][:, js, 1], op=ALU.add)
+            for js in halves:
+                nc.vector.tensor_tensor(out=total[m][:, js], in0=sums[m][:, js], in1=ex[m][:, js], op=ALU.add)
+
+        def take_log(m, a, b):
             nc.scalar.activation(out=logs[m][:, a:b], in_=total[m][:, a:b], func=ACT.Ln)
-            nc.vector.tensor_tensor(out=res[m][:, a:b], in0=logs[m][:, a:b], in1=h_ps[m][hf][:], op=ALU.subtract)
+
+        def finish(m, a, b):
+            hf = a // HALF
+            nc.vector.tensor_tensor(
+                out=res[m][:, a:b], in0=logs[m][:, a:b], in1=h_ps[m][hf][:, a - hf * HALF : b - hf * HALF], op=ALU.subtract
+            )
             nc.sync.dma_start(out=out[m * P : (m + 1) * P, a:b], in_=res[m][:, a:b])
 
-        gather_members(0)
         for m in range(N // P):
-            if m + 1 < N // P:
-                gather_members(m + 1)
-            for hf in range(2):
-                add_members(m, hf * HALF, (hf + 1) * HALF)
-            for hf in range(2):
-                finish(m, hf)
+            for blk in range(S // P):
+                a, b = blk * P, (blk + 1) * P
+                if blk % 2 == 1 or (m, blk) == (3, 2):
+                    gather_members("scalar", m, a, b)
+                else:
+                    gather_members("vector", m, a, b)
+                if m in TENSOR_TILES:
+                    add_turned(m, blk)
+            if m == 1:
+                copy_h(1)
+        for m in (2, 3):
+            add_members(m)
+        for m in (0, 2, 1, 3):
+            if m in TENSOR_TILES:
+                log_turned(m)
+            else:
+                take_log(m, 0, S)
+        for m in (0, 2, 1, 3):
+            if m in TENSOR_TILES:
+                finish_turned(m)
+            else:
+                for hf in range(2):
+                    finish(m, hf * HALF, (hf + 1) * HALF)

@@ -25,7 +25,9 @@ SPARE = 32
 PIECE = 512
 Z_CHUNKS = ((0, 256), (256, 512))
 TENSOR_TILES = (0, 1)
+GATED_TAG = {(0, 1): "w2_raw", (1, 0): "w2_raw", (1, 1): "larger0"}
 Y_ON_VECTOR = (1, 2)
+OTHER_ON_VECTOR = ((0, 0),)
 
 
 def tile_picked_mixingmaxglse_none_p_kernel(
@@ -125,8 +127,11 @@ def tile_picked_mixingmaxglse_none_p_kernel(
         y = [sb("y%d" % t, [P, S], F32) for t in range(PACK)]
         gate = [sb("gate%d" % c, [P, PACK, b - a], F32) for c, (a, b) in enumerate(Z_CHUNKS)]
         other = [sb("other%d" % c, [P, PACK, b - a], F32) for c, (a, b) in enumerate(Z_CHUNKS)]
-        gated = [sb("gated%d" % c, [P, PACK, b - a], F32, tag="w2_raw") for c, (a, b) in enumerate(Z_CHUNKS)]
         larger = [sb("larger%d" % c, [P, PACK, b - a], F32) for c, (a, b) in enumerate(Z_CHUNKS)]
+        gated = {}
+        for c, (a, b) in enumerate(Z_CHUNKS):
+            for u in range(2):
+                gated[c, u] = sb("gated%d_%d" % (c, u), [P, 2, b - a], F32, tag=GATED_TAG.get((c, u)))
         z_bf = [sb("z_bf%d" % c, [P, b - a, PACK], BF16) for c, (a, b) in enumerate(Z_CHUNKS)]
         z_codes = [sb("z_codes%d" % c, [P, b - a], U32) for c, (a, b) in enumerate(Z_CHUNKS)]
         z_scales = [sb("z_scales%d" % c, [P, b - a], U8) for c, (a, b) in enumerate(Z_CHUNKS)]
@@ -143,14 +148,18 @@ def tile_picked_mixingmaxglse_none_p_kernel(
 
         def gather_other(c, t):
             a, b = Z_CHUNKS[c]
-            nc.scalar.activation(out=other[c][:, t, :], in_=y[t][:].indirect(cols(n2_t, a, b)), func=ACT.Copy)
+            src = y[t][:].indirect(cols(n2_t, a, b))
+            if (c, t) in OTHER_ON_VECTOR:
+                nc.vector.tensor_copy(out=other[c][:, t, :], in_=src)
+            else:
+                nc.scalar.activation(out=other[c][:, t, :], in_=src, func=ACT.Copy)
 
         def apply_gate(c, t):
             a, b = Z_CHUNKS[c]
-            nc.vector.tensor_tensor(out=gated[c][:, t, :], in0=gate[c][:, t, :], in1=y[t][:, a:b], op=ALU.mult)
+            nc.vector.tensor_tensor(out=gated[c, t // 2][:, t % 2, :], in0=gate[c][:, t, :], in1=y[t][:, a:b], op=ALU.mult)
 
         def take_larger(c, t):
-            nc.vector.tensor_tensor(out=larger[c][:, t, :], in0=gated[c][:, t, :], in1=other[c][:, t, :], op=ALU.max)
+            nc.vector.tensor_tensor(out=larger[c][:, t, :], in0=gated[c, t // 2][:, t % 2, :], in1=other[c][:, t, :], op=ALU.max)
 
         def make_z(c):
             a, b = Z_CHUNKS[c]
@@ -162,20 +171,23 @@ def tile_picked_mixingmaxglse_none_p_kernel(
             )
             quantize(z_codes[c][:], z_scales[c][:], z_bf[c][:].rearrange("p j t -> p (j t)"))
 
-        def prepare_weight(name, raw):
+        def prepare_weight(name, raw, on_gpsimd):
             bf = sb(name + "_bf", [P, N, PACK], BF16)
             codes = sb(name + "_codes", [P, N], U32)
             scales = sb(name + "_scales", [P, N], U8)
-            nc.vector.tensor_copy(
-                out=bf[:].rearrange("p (g i) j -> p g j i", i=4),
-                in_=raw[:].rearrange("p j (g i) -> p g j i", i=4),
-            )
+            if on_gpsimd:
+                nc.gpsimd.tensor_copy(out=bf[:], in_=raw[:].rearrange("p j n -> p n j"))
+            else:
+                nc.vector.tensor_copy(
+                    out=bf[:].rearrange("p (g i) j -> p g j i", i=4),
+                    in_=raw[:].rearrange("p j (g i) -> p g j i", i=4),
+                )
             return bf, codes, scales
 
         for t in Y_ON_VECTOR:
             copy_y(t)
-        w3_bf, w3_codes, w3_scales = prepare_weight("w3", w3_raw)
-        w2_bf, w2_codes, w2_scales = prepare_weight("w2", w2_raw)
+        w3_bf, w3_codes, w3_scales = prepare_weight("w3", w3_raw, True)
+        w2_bf, w2_codes, w2_scales = prepare_weight("w2", w2_raw, False)
         quantize(w3_codes[:], w3_scales[:], w3_bf[:].rearrange("p n j -> p (n j)"))
         quantize(w2_codes[:], w2_scales[:], w2_bf[:].rearrange("p n j -> p (n j)"))
         for t in range(PACK):
@@ -224,16 +236,17 @@ def tile_picked_mixingmaxglse_none_p_kernel(
                     start=False,
                     stop=(b == (hf + 1) * HALF),
                 )
-        h_sb = {m: sb("h_sb%d" % m, [P, S], F32) for m in TENSOR_TILES}
+        h_sb = {m: sb("h_sb%d" % m, [P, S], F32, tag=("z_bf1", "larger1")[m]) for m in TENSOR_TILES}
 
         def copy_h(hf):
             for m in TENSOR_TILES:
                 nc.vector.tensor_copy(out=h_sb[m][:, hf * HALF : (hf + 1) * HALF], in_=h_ps[m][hf][:])
 
-        copy_h(0)
         for hf in range(2):
             for m in range(N // P):
                 nc.scalar.activation(out=ex[m][:, hf * HALF : (hf + 1) * HALF], in_=h_ps[m][hf][:], func=ACT.Exp)
+            if hf == 0:
+                copy_h(0)
 
         members = [sb("members%d" % m, [P, S, MEMBERS], F32) for m in range(N // P)]
         pairs = [sb("pairs%d" % m, [P, S, 2], F32) for m in range(N // P)]
@@ -268,14 +281,13 @@ def tile_picked_mixingmaxglse_none_p_kernel(
             nc.vector.tensor_tensor(out=res[m][:], in0=back[m][:], in1=h_sb[m][:], op=ALU.subtract)
             nc.sync.dma_start(out=out[m * P : (m + 1) * P, :], in_=res[m][:])
 
-        def add_members(m):
-            halves = [slice(hf * HALF, (hf + 1) * HALF) for hf in range(2)]
+        def add_members(engine, m, halves):
             for js in halves:
-                nc.vector.tensor_tensor(out=pairs[m][:, js, :], in0=members[m][:, js, 0:2], in1=members[m][:, js, 2:4], op=ALU.add)
+                engine.tensor_tensor(out=pairs[m][:, js, :], in0=members[m][:, js, 0:2], in1=members[m][:, js, 2:4], op=ALU.add)
             for js in halves:
-                nc.vector.tensor_tensor(out=sums[m][:, js], in0=pairs[m][:, js, 0], in1=pairs[m][:, js, 1], op=ALU.add)
+                engine.tensor_tensor(out=sums[m][:, js], in0=pairs[m][:, js, 0], in1=pairs[m][:, js, 1], op=ALU.add)
             for js in halves:
-                nc.vector.tensor_tensor(out=total[m][:, js], in0=sums[m][:, js], in1=ex[m][:, js], op=ALU.add)
+                engine.tensor_tensor(out=total[m][:, js], in0=sums[m][:, js], in1=ex[m][:, js], op=ALU.add)
 
         def take_log(m, a, b):
             nc.scalar.activation(out=logs[m][:, a:b], in_=total[m][:, a:b], func=ACT.Ln)
@@ -287,25 +299,27 @@ def tile_picked_mixingmaxglse_none_p_kernel(
             )
             nc.sync.dma_start(out=out[m * P : (m + 1) * P, a:b], in_=res[m][:, a:b])
 
-        for m in range(N // P):
-            for blk in range(S // P):
+        for m, hf in ((0, 0), (2, 0), (0, 1), (2, 1), (1, 0), (1, 1), (3, 0), (3, 1)):
+            for engine, blk in (("vector", 2 * hf), ("scalar", 2 * hf + 1)):
                 a, b = blk * P, (blk + 1) * P
-                if blk % 2 == 1 or (m, blk) == (3, 2):
-                    gather_members("scalar", m, a, b)
-                else:
-                    gather_members("vector", m, a, b)
+                if (m, blk) == (3, 3) and 0:
+                    gather_members("vector", m, a, a + 0)
+                    a = a + 0
+                gather_members(engine, m, a, b)
                 if m in TENSOR_TILES:
                     add_turned(m, blk)
-            if m == 1:
+            if (m, hf) == (1, 1):
                 copy_h(1)
-        for m in (2, 3):
-            add_members(m)
+        first, second = slice(0, HALF), slice(HALF, S)
+        add_members(nc.gpsimd, 2, [first])
+        add_members(nc.gpsimd, 2, [second])
+        add_members(nc.vector, 3, [first, second])
         for m in (0, 2, 1, 3):
             if m in TENSOR_TILES:
                 log_turned(m)
             else:
                 take_log(m, 0, S)
-        for m in (0, 2, 1, 3):
+        for m in (2, 0, 1, 3):
             if m in TENSOR_TILES:
                 finish_turned(m)
             else:

@@ -25,8 +25,8 @@ SPARE = 32
 PIECE = 512
 Z_CHUNKS = ((0, 256), (256, 512))
 TENSOR_TILES = (0, 1)
-GATED_TAG = {(0, 1): "w2_raw", (1, 0): "w2_raw", (1, 1): "larger0"}
-Y_ON_VECTOR = (1, 2)
+GATED_TAG = {(0, 0): "w3_raw", (0, 1): "w2_raw", (1, 0): "w2_raw", (1, 1): "larger0"}
+Y_ON_VECTOR = (1,)
 OTHER_ON_VECTOR = ((0, 0),)
 
 
@@ -186,7 +186,7 @@ def tile_picked_mixingmaxglse_none_p_kernel(
 
         for t in Y_ON_VECTOR:
             copy_y(t)
-        w3_bf, w3_codes, w3_scales = prepare_weight("w3", w3_raw, True)
+        w3_bf, w3_codes, w3_scales = prepare_weight("w3", w3_raw, False)
         w2_bf, w2_codes, w2_scales = prepare_weight("w2", w2_raw, False)
         quantize(w3_codes[:], w3_scales[:], w3_bf[:].rearrange("p n j -> p (n j)"))
         quantize(w2_codes[:], w2_scales[:], w2_bf[:].rearrange("p n j -> p (n j)"))
@@ -225,7 +225,7 @@ def tile_picked_mixingmaxglse_none_p_kernel(
                 )
         for c, (a, b) in enumerate(Z_CHUNKS):
             hf = a // HALF
-            for m in range(N // P):
+            for m in (0, 2, 1, 3):
                 mc = slice(m * P, (m + 1) * P)
                 nc.tensor.matmul_mx(
                     out=h_ps[m][hf][:, a - hf * HALF : b - hf * HALF],
@@ -243,17 +243,17 @@ def tile_picked_mixingmaxglse_none_p_kernel(
                 nc.vector.tensor_copy(out=h_sb[m][:, hf * HALF : (hf + 1) * HALF], in_=h_ps[m][hf][:])
 
         for hf in range(2):
-            for m in range(N // P):
+            for m in (0, 2, 1, 3):
                 nc.scalar.activation(out=ex[m][:, hf * HALF : (hf + 1) * HALF], in_=h_ps[m][hf][:], func=ACT.Exp)
             if hf == 0:
                 copy_h(0)
 
         members = [sb("members%d" % m, [P, S, MEMBERS], F32) for m in range(N // P)]
-        pairs = [sb("pairs%d" % m, [P, S, 2], F32) for m in range(N // P)]
+        pairs = {(m, hf): sb("pairs%d_%d" % (m, hf), [P, HALF, 2], F32, tag="pairs2" if m == 2 else None) for m in (2, 3) for hf in range(2)}
         sums = [sb("sums%d" % m, [P, S], F32) for m in range(N // P)]
         total = [sb("total%d" % m, [P, S], F32) for m in range(N // P)]
-        logs = [sb("logs%d" % m, [P, S], F32) for m in range(N // P)]
-        res = [sb("res%d" % m, [P, S], F32) for m in range(N // P)]
+        logs = [sb("logs%d" % m, [P, S], F32, tag={1: "sums2", 3: "total2"}.get(m)) for m in range(N // P)]
+        res = [sb("res%d" % m, [P, S], F32, tag="logs2" if m == 0 else None) for m in range(N // P)]
         turned = {m: psum.tile([P, S], F32, name="turned%d" % m, tag="bank%d" % (m + 4)) for m in TENSOR_TILES}
         back = {m: psum.tile([P, S], F32, name="back%d" % m, tag="bank%d" % m) for m in TENSOR_TILES}
 
@@ -282,11 +282,14 @@ def tile_picked_mixingmaxglse_none_p_kernel(
             nc.sync.dma_start(out=out[m * P : (m + 1) * P, :], in_=res[m][:])
 
         def add_members(engine, m, halves):
-            for js in halves:
-                engine.tensor_tensor(out=pairs[m][:, js, :], in0=members[m][:, js, 0:2], in1=members[m][:, js, 2:4], op=ALU.add)
-            for js in halves:
-                engine.tensor_tensor(out=sums[m][:, js], in0=pairs[m][:, js, 0], in1=pairs[m][:, js, 1], op=ALU.add)
-            for js in halves:
+            for hf in halves:
+                js = slice(hf * HALF, (hf + 1) * HALF)
+                engine.tensor_tensor(out=pairs[m, hf][:], in0=members[m][:, js, 0:2], in1=members[m][:, js, 2:4], op=ALU.add)
+            for hf in halves:
+                js = slice(hf * HALF, (hf + 1) * HALF)
+                engine.tensor_tensor(out=sums[m][:, js], in0=pairs[m, hf][:, :, 0], in1=pairs[m, hf][:, :, 1], op=ALU.add)
+            for hf in halves:
+                js = slice(hf * HALF, (hf + 1) * HALF)
                 engine.tensor_tensor(out=total[m][:, js], in0=sums[m][:, js], in1=ex[m][:, js], op=ALU.add)
 
         def take_log(m, a, b):
@@ -302,18 +305,17 @@ def tile_picked_mixingmaxglse_none_p_kernel(
         for m, hf in ((0, 0), (2, 0), (0, 1), (2, 1), (1, 0), (1, 1), (3, 0), (3, 1)):
             for engine, blk in (("vector", 2 * hf), ("scalar", 2 * hf + 1)):
                 a, b = blk * P, (blk + 1) * P
-                if (m, blk) == (3, 3) and 0:
-                    gather_members("vector", m, a, a + 0)
-                    a = a + 0
+                if (m, blk) == (3, 3):
+                    gather_members("vector", m, a, a + 32)
+                    a = a + 32
                 gather_members(engine, m, a, b)
                 if m in TENSOR_TILES:
                     add_turned(m, blk)
             if (m, hf) == (1, 1):
                 copy_h(1)
-        first, second = slice(0, HALF), slice(HALF, S)
-        add_members(nc.gpsimd, 2, [first])
-        add_members(nc.gpsimd, 2, [second])
-        add_members(nc.vector, 3, [first, second])
+        add_members(nc.gpsimd, 2, [0])
+        add_members(nc.gpsimd, 2, [1])
+        add_members(nc.vector, 3, [0, 1])
         for m in (0, 2, 1, 3):
             if m in TENSOR_TILES:
                 log_turned(m)

@@ -19,15 +19,29 @@ ALU = mybir.AluOpType
 P = 128
 PACK = 4
 STRIPE = 16
+LINE = 4
 HALF = S // 2
 MEMBERS = W // S
+ROW_TILES = N // P
 SPARE = 32
-PIECE = 512
-Z_CHUNKS = ((0, 256), (256, 512))
-TENSOR_TILES = (0, 1)
-GATED_TAG = {(0, 0): "w3_raw", (0, 1): "w2_raw", (1, 0): "w2_raw", (1, 1): "larger0"}
-Y_ON_VECTOR = (1,)
-OTHER_ON_VECTOR = ((0, 0),)
+Y_ON_VECTOR = 1
+N2_ON_VECTOR = (0, 0)
+TURNED_TILES = (0, 1, 2)
+PAIRED_TILES = (1, 2)
+DIRECT_TILE = 3
+LAST_SHARE = 32
+
+
+def half(hf):
+    return slice(hf * HALF, (hf + 1) * HALF)
+
+
+def block(blk):
+    return slice(blk * P, (blk + 1) * P)
+
+
+def entries(list_tile, first, last):
+    return list_tile[:, first // STRIPE : last // STRIPE]
 
 
 def tile_picked_mixingmaxglse_none_p_kernel(
@@ -38,26 +52,42 @@ def tile_picked_mixingmaxglse_none_p_kernel(
         keep = ctx.enter_context(tc.tile_pool(name="keep", bufs=1))
         psum = ctx.enter_context(tc.psum_pool(name="psum", bufs=1))
 
-        def sb(name, shape, dtype, tag=None):
-            return keep.tile(shape, dtype, name=name, tag=tag or name, align_bytes=64)
+        def sb(name, shape, dtype, after=None):
+            return keep.tile(shape, dtype, name=name, tag=after or name, align_bytes=64)
+
+        def bank(name, width, number):
+            return psum.tile([P, width], F32, name=name, tag="bank%d" % number)
+
+        def quantize(codes, scales, values):
+            nc.vector.quantize_mx(out=codes.bitcast(FP8X4), scales=scales, in_=values)
+
+        def product(dst, w_codes, w_scales, x_codes, x_bytes, start, stop):
+            nc.tensor.matmul_mx(
+                out=dst,
+                lhsT=w_codes.bitcast(FP8X4),
+                lhsT_scale=w_scales,
+                rhs=x_codes.bitcast(FP8X4),
+                rhs_scale=x_bytes,
+                start=start,
+                stop=stop,
+            )
 
         offs_t = sb("offs_t", [P, S // STRIPE], U16)
         two_t = sb("two_t", [P, S // STRIPE], U16)
         n1_t = sb("n1_t", [P, S // STRIPE], U16)
         n2_t = sb("n2_t", [P, S // STRIPE], U16)
         n3_t = sb("n3_t", [P, W // STRIPE], U16)
-        xw = sb("xw", [P, T], U32)
-        xs = sb("xs", [P, T], U8)
+        words = sb("words", [P, T], U32)
+        scale_bytes = sb("scale_bytes", [P, T], U8)
         w1_raw = sb("w1_raw", [P, PACK, H], F32)
         w2_raw = sb("w2_raw", [P, PACK, N], F32)
         w3_raw = sb("w3_raw", [P, PACK, N], F32)
         gain = sb("gain", [P, PACK], F32)
-        ex = [sb("ex%d" % m, [P, S + SPARE], F32) for m in range(N // P)]
+        ex = [sb("ex%d" % m, [P, S + SPARE], F32) for m in range(ROW_TILES)]
 
-        nc.gpsimd.memset(xs[:].bitcast(I32), 0)
-        for m in range(N // P):
+        nc.gpsimd.memset(scale_bytes[:].bitcast(I32), 0)
+        for m in range(ROW_TILES):
             nc.gpsimd.memset(ex[m][:, S:], 0.0)
-
         ident = sb("ident", [P, P], F32)
         make_identity(nc, ident[:])
 
@@ -68,11 +98,11 @@ def tile_picked_mixingmaxglse_none_p_kernel(
         nc.sync.dma_start(two_t[:], two)
         for q in range(4):
             nc.sync.dma_start(
-                out=xs[32 * q : 32 * q + 4, :].bitcast(I32),
+                out=scale_bytes[32 * q : 32 * q + 4, :].bitcast(I32),
                 in_=x_scales[0, 4 * q : 4 * q + 4, :].bitcast(I32),
             )
         nc.sync.dma_start(out=w1_raw[:], in_=w1.rearrange("(p j) c -> p j c", j=PACK))
-        nc.sync.dma_start(out=xw[:].bitcast(I32), in_=x_words[0].rearrange("p n t -> p (n t)").bitcast(I32))
+        nc.sync.dma_start(out=words[:].bitcast(I32), in_=x_words[0].rearrange("p n j -> p (n j)").bitcast(I32))
         nc.sync.dma_start(n1_t[:], n1)
         nc.sync.dma_start(n2_t[:], n2)
         nc.sync.dma_start(out=w3_raw[:], in_=w3.rearrange("(p j) c -> p j c", j=PACK))
@@ -80,250 +110,208 @@ def tile_picked_mixingmaxglse_none_p_kernel(
         nc.sync.dma_start(out=w2_raw[:], in_=w2.rearrange("(p j) c -> p j c", j=PACK))
         nc.sync.dma_start(n3_t[:], n3)
 
-        def cols(lst, a, b):
-            return lst[:, a // STRIPE : b // STRIPE]
-
         w1_codes = [sb("w1_codes%d" % u, [P, 2 * P], U32) for u in range(2)]
         w1_scales = [sb("w1_scales%d" % u, [P, 2 * P], U8) for u in range(2)]
         w1_bf = [sb("w1_bf%d" % u, [P, 2, P, PACK], BF16) for u in range(2)]
-
-        xa_s = sb("xa_s", [P, S], U8)
-        xb_s = sb("xb_s", [P, S], U8)
-        xa_w = [sb("xa_w%d" % c, [P, HALF], U32) for c in range(2)]
-        xb_w = sb("xb_w", [P, S], U32)
-        nc.vector.tensor_copy(out=xa_s[:], in_=xs[:].indirect(offs_t[:]))
-        nc.vector.tensor_copy(out=xb_s[:], in_=xs[:].indirect(two_t[:]))
-
-        def quantize(codes, scales, values):
-            nc.vector.quantize_mx(out=codes.bitcast(FP8X4), scales=scales, in_=values)
+        xa_bytes = sb("xa_bytes", [P, S], U8)
+        xb_bytes = sb("xb_bytes", [P, S], U8)
+        xa_words = [sb("xa_words%d" % hf, [P, HALF], U32) for hf in range(2)]
+        xb_words = sb("xb_words", [P, S], U32)
+        nc.vector.tensor_copy(out=xa_bytes[:], in_=scale_bytes[:].indirect(offs_t[:]))
+        nc.vector.tensor_copy(out=xb_bytes[:], in_=scale_bytes[:].indirect(two_t[:]))
 
         for u, cast in enumerate((nc.scalar.copy, nc.vector.tensor_copy)):
             cast(
-                out=w1_bf[u][:].rearrange("p t m j -> p m j t"),
-                in_=w1_raw[:].rearrange("p j (m t) -> p m j t", t=PACK)[:, :, :, 2 * u : 2 * u + 2],
+                out=w1_bf[u][:].rearrange("p t c j -> p c j t"),
+                in_=w1_raw[:].rearrange("p j (c t) -> p c j t", t=PACK)[:, :, :, 2 * u : 2 * u + 2],
             )
         for u in range(2):
-            quantize(w1_codes[u][:], w1_scales[u][:], w1_bf[u][:].rearrange("p t m j -> p (t m j)"))
+            quantize(w1_codes[u][:], w1_scales[u][:], w1_bf[u][:].rearrange("p t c j -> p (t c j)"))
+        for hf in range(2):
+            nc.vector.tensor_copy(out=xa_words[hf][:], in_=words[:].indirect(entries(offs_t, hf * HALF, (hf + 1) * HALF)))
+        nc.vector.tensor_copy(out=xb_words[:], in_=words[:].indirect(two_t[:]))
 
-        for c in range(2):
-            nc.vector.tensor_copy(out=xa_w[c][:], in_=xw[:].indirect(cols(offs_t, c * HALF, (c + 1) * HALF)))
-        nc.vector.tensor_copy(out=xb_w[:], in_=xw[:].indirect(two_t[:]))
-
-        y_ps = [psum.tile([P, S], F32, name="y_ps%d" % t, tag="bank%d" % t) for t in range(PACK)]
-        for pair in range(2):
-            for c in range(2):
-                for t in (2 * pair, 2 * pair + 1):
-                    mc = slice((t % 2) * P, (t % 2 + 1) * P)
-                    nc.tensor.matmul_mx(
-                        out=y_ps[t][:, c * HALF : (c + 1) * HALF],
-                        lhsT=w1_codes[pair][:, mc].bitcast(FP8X4),
-                        lhsT_scale=w1_scales[pair][:, mc],
-                        rhs=xa_w[c][:].bitcast(FP8X4),
-                        rhs_scale=xa_s[:, c * HALF : (c + 1) * HALF],
-                        start=True,
-                        stop=True,
+        y_ps = [bank("y_ps%d" % t, S, t) for t in range(PACK)]
+        for u in range(2):
+            for hf in range(2):
+                for t in (2 * u, 2 * u + 1):
+                    cs = block(t % 2)
+                    product(
+                        y_ps[t][:, half(hf)], w1_codes[u][:, cs], w1_scales[u][:, cs],
+                        xa_words[hf][:], xa_bytes[:, half(hf)], True, True,
                     )
 
         y = [sb("y%d" % t, [P, S], F32) for t in range(PACK)]
-        gate = [sb("gate%d" % c, [P, PACK, b - a], F32) for c, (a, b) in enumerate(Z_CHUNKS)]
-        other = [sb("other%d" % c, [P, PACK, b - a], F32) for c, (a, b) in enumerate(Z_CHUNKS)]
-        larger = [sb("larger%d" % c, [P, PACK, b - a], F32) for c, (a, b) in enumerate(Z_CHUNKS)]
-        gated = {}
-        for c, (a, b) in enumerate(Z_CHUNKS):
-            for u in range(2):
-                gated[c, u] = sb("gated%d_%d" % (c, u), [P, 2, b - a], F32, tag=GATED_TAG.get((c, u)))
-        z_bf = [sb("z_bf%d" % c, [P, b - a, PACK], BF16) for c, (a, b) in enumerate(Z_CHUNKS)]
-        z_codes = [sb("z_codes%d" % c, [P, b - a], U32) for c, (a, b) in enumerate(Z_CHUNKS)]
-        z_scales = [sb("z_scales%d" % c, [P, b - a], U8) for c, (a, b) in enumerate(Z_CHUNKS)]
+        gate = [sb("gate%d" % hf, [P, PACK, HALF], F32) for hf in range(2)]
+        other = [sb("other%d" % hf, [P, PACK, HALF], F32) for hf in range(2)]
+        larger = [sb("larger%d" % hf, [P, PACK, HALF], F32) for hf in range(2)]
+        z_bf = [sb("z_bf%d" % hf, [P, HALF, PACK], BF16) for hf in range(2)]
+        z_codes = [sb("z_codes%d" % hf, [P, HALF], U32) for hf in range(2)]
+        z_scales = [sb("z_scales%d" % hf, [P, HALF], U8) for hf in range(2)]
 
         def copy_y(t):
-            if t in Y_ON_VECTOR:
+            if t == Y_ON_VECTOR:
                 nc.vector.tensor_copy(out=y[t][:], in_=y_ps[t][:])
             else:
                 nc.scalar.copy(out=y[t][:], in_=y_ps[t][:])
 
-        def gather_gate(c, t):
-            a, b = Z_CHUNKS[c]
-            nc.scalar.activation(out=gate[c][:, t, :], in_=y[t][:].indirect(cols(n1_t, a, b)), func=ACT.Sigmoid)
+        def gather_gate(hf, t):
+            src = y[t][:].indirect(entries(n1_t, hf * HALF, (hf + 1) * HALF))
+            nc.scalar.activation(out=gate[hf][:, t, :], in_=src, func=ACT.Sigmoid)
 
-        def gather_other(c, t):
-            a, b = Z_CHUNKS[c]
-            src = y[t][:].indirect(cols(n2_t, a, b))
-            if (c, t) in OTHER_ON_VECTOR:
-                nc.vector.tensor_copy(out=other[c][:, t, :], in_=src)
+        def gather_other(hf, t):
+            src = y[t][:].indirect(entries(n2_t, hf * HALF, (hf + 1) * HALF))
+            if (hf, t) == N2_ON_VECTOR:
+                nc.vector.tensor_copy(out=other[hf][:, t, :], in_=src)
             else:
-                nc.scalar.activation(out=other[c][:, t, :], in_=src, func=ACT.Copy)
+                nc.scalar.activation(out=other[hf][:, t, :], in_=src, func=ACT.Copy)
 
-        def apply_gate(c, t):
-            a, b = Z_CHUNKS[c]
-            nc.vector.tensor_tensor(out=gated[c, t // 2][:, t % 2, :], in0=gate[c][:, t, :], in1=y[t][:, a:b], op=ALU.mult)
+        def apply_gate(hf, t):
+            dst = gated[2 * hf + t // 2][:, t % 2, :]
+            nc.vector.tensor_tensor(out=dst, in0=gate[hf][:, t, :], in1=y[t][:, half(hf)], op=ALU.mult)
 
-        def take_larger(c, t):
-            nc.vector.tensor_tensor(out=larger[c][:, t, :], in0=gated[c, t // 2][:, t % 2, :], in1=other[c][:, t, :], op=ALU.max)
+        def take_larger(hf, t):
+            src = gated[2 * hf + t // 2][:, t % 2, :]
+            nc.vector.tensor_tensor(out=larger[hf][:, t, :], in0=src, in1=other[hf][:, t, :], op=ALU.max)
 
-        def make_z(c):
-            a, b = Z_CHUNKS[c]
+        def make_z(hf):
             nc.vector.tensor_tensor(
-                out=z_bf[c][:].rearrange("p (g i) t -> p g t i", i=4),
-                in0=larger[c][:].rearrange("p t (g i) -> p g t i", i=4),
-                in1=gain[:].unsqueeze(1).unsqueeze(3).to_broadcast([P, (b - a) // 4, PACK, 4]),
+                out=z_bf[hf][:].rearrange("p (g i) t -> p g t i", i=LINE),
+                in0=larger[hf][:].rearrange("p t (g i) -> p g t i", i=LINE),
+                in1=gain[:].unsqueeze(1).unsqueeze(3).to_broadcast([P, HALF // LINE, PACK, LINE]),
                 op=ALU.mult,
             )
-            quantize(z_codes[c][:], z_scales[c][:], z_bf[c][:].rearrange("p j t -> p (j t)"))
+            quantize(z_codes[hf][:], z_scales[hf][:], z_bf[hf][:].rearrange("p s t -> p (s t)"))
 
-        def prepare_weight(name, raw, on_gpsimd):
+        def round_weight(name, raw):
             bf = sb(name + "_bf", [P, N, PACK], BF16)
             codes = sb(name + "_codes", [P, N], U32)
             scales = sb(name + "_scales", [P, N], U8)
-            if on_gpsimd:
-                nc.gpsimd.tensor_copy(out=bf[:], in_=raw[:].rearrange("p j n -> p n j"))
-            else:
-                nc.vector.tensor_copy(
-                    out=bf[:].rearrange("p (g i) j -> p g j i", i=4),
-                    in_=raw[:].rearrange("p j (g i) -> p g j i", i=4),
-                )
+            nc.vector.tensor_copy(
+                out=bf[:].rearrange("p (g i) j -> p g j i", i=LINE),
+                in_=raw[:].rearrange("p j (g i) -> p g j i", i=LINE),
+            )
             return bf, codes, scales
 
-        for t in Y_ON_VECTOR:
-            copy_y(t)
-        w3_bf, w3_codes, w3_scales = prepare_weight("w3", w3_raw, False)
-        w2_bf, w2_codes, w2_scales = prepare_weight("w2", w2_raw, False)
+        copy_y(Y_ON_VECTOR)
+        w3_bf, w3_codes, w3_scales = round_weight("w3", w3_raw)
+        w2_bf, w2_codes, w2_scales = round_weight("w2", w2_raw)
         quantize(w3_codes[:], w3_scales[:], w3_bf[:].rearrange("p n j -> p (n j)"))
         quantize(w2_codes[:], w2_scales[:], w2_bf[:].rearrange("p n j -> p (n j)"))
+        taken_over = ("w3_raw", "w2_raw", "w2_raw", "larger0")
+        gated = [sb("gated%d" % i, [P, 2, HALF], F32, after=name) for i, name in enumerate(taken_over)]
         for t in range(PACK):
-            if t not in Y_ON_VECTOR:
+            if t != Y_ON_VECTOR:
                 copy_y(t)
             gather_gate(0, t)
             gather_other(0, t)
             apply_gate(0, t)
             take_larger(0, t)
         make_z(0)
-        for c in range(1, len(Z_CHUNKS)):
-            for t in range(PACK):
-                gather_gate(c, t)
-                apply_gate(c, t)
-            for t in range(PACK):
-                gather_other(c, t)
-                take_larger(c, t)
-            make_z(c)
+        for t in range(PACK):
+            gather_gate(1, t)
+            apply_gate(1, t)
+        for t in range(PACK):
+            gather_other(1, t)
+            take_larger(1, t)
+        make_z(1)
 
-        h_ps = [
-            [psum.tile([P, HALF], F32, name="h_ps%d_%d" % (m, hf), tag="bank%d" % (m + 4 * (1 - hf))) for hf in range(2)]
-            for m in range(N // P)
-        ]
+        h_ps = [[bank("h_ps%d_%d" % (m, hf), HALF, m + PACK * (1 - hf)) for hf in range(2)] for m in range(ROW_TILES)]
         for hf in range(2):
-            for m in range(N // P):
-                mc = slice(m * P, (m + 1) * P)
-                nc.tensor.matmul_mx(
-                    out=h_ps[m][hf][:],
-                    lhsT=w3_codes[:, mc].bitcast(FP8X4),
-                    lhsT_scale=w3_scales[:, mc],
-                    rhs=xb_w[:, hf * HALF : (hf + 1) * HALF].bitcast(FP8X4),
-                    rhs_scale=xb_s[:, hf * HALF : (hf + 1) * HALF],
-                    start=True,
-                    stop=False,
+            for m in range(ROW_TILES):
+                product(
+                    h_ps[m][hf][:], w3_codes[:, block(m)], w3_scales[:, block(m)],
+                    xb_words[:, half(hf)], xb_bytes[:, half(hf)], True, False,
                 )
-        for c, (a, b) in enumerate(Z_CHUNKS):
-            hf = a // HALF
-            for m in (0, 2, 1, 3):
-                mc = slice(m * P, (m + 1) * P)
-                nc.tensor.matmul_mx(
-                    out=h_ps[m][hf][:, a - hf * HALF : b - hf * HALF],
-                    lhsT=w2_codes[:, mc].bitcast(FP8X4),
-                    lhsT_scale=w2_scales[:, mc],
-                    rhs=z_codes[c][:].bitcast(FP8X4),
-                    rhs_scale=z_scales[c][:],
-                    start=False,
-                    stop=(b == (hf + 1) * HALF),
+        for hf in range(2):
+            for m in range(ROW_TILES):
+                product(
+                    h_ps[m][hf][:], w2_codes[:, block(m)], w2_scales[:, block(m)],
+                    z_codes[hf][:], z_scales[hf][:], False, True,
                 )
-        h_sb = {m: sb("h_sb%d" % m, [P, S], F32, tag=("z_bf1", "larger1")[m]) for m in TENSOR_TILES}
+
+        h_sb = sb("h_sb", [P, len(TURNED_TILES), S], F32, after="z_bf1")
 
         def copy_h(hf):
-            for m in TENSOR_TILES:
-                nc.vector.tensor_copy(out=h_sb[m][:, hf * HALF : (hf + 1) * HALF], in_=h_ps[m][hf][:])
+            for m in TURNED_TILES:
+                nc.vector.tensor_copy(out=h_sb[:, m, half(hf)], in_=h_ps[m][hf][:])
 
         for hf in range(2):
-            for m in (0, 2, 1, 3):
-                nc.scalar.activation(out=ex[m][:, hf * HALF : (hf + 1) * HALF], in_=h_ps[m][hf][:], func=ACT.Exp)
+            for m in range(ROW_TILES):
+                nc.scalar.activation(out=ex[m][:, half(hf)], in_=h_ps[m][hf][:], func=ACT.Exp)
             if hf == 0:
                 copy_h(0)
 
-        members = [sb("members%d" % m, [P, S, MEMBERS], F32) for m in range(N // P)]
-        pairs = {(m, hf): sb("pairs%d_%d" % (m, hf), [P, HALF, 2], F32, tag="pairs2" if m == 2 else None) for m in (2, 3) for hf in range(2)}
-        sums = [sb("sums%d" % m, [P, S], F32) for m in range(N // P)]
-        total = [sb("total%d" % m, [P, S], F32) for m in range(N // P)]
-        logs = [sb("logs%d" % m, [P, S], F32, tag={1: "sums2", 3: "total2"}.get(m)) for m in range(N // P)]
-        res = [sb("res%d" % m, [P, S], F32, tag="logs2" if m == 0 else None) for m in range(N // P)]
-        turned = {m: psum.tile([P, S], F32, name="turned%d" % m, tag="bank%d" % (m + 4)) for m in TENSOR_TILES}
-        back = {m: psum.tile([P, S], F32, name="back%d" % m, tag="bank%d" % m) for m in TENSOR_TILES}
+        members = [sb("members%d" % m, [P, S, MEMBERS], F32) for m in range(ROW_TILES)]
+        pairs = {
+            (m, hf): sb("pairs%d_%d" % (m, hf), [P, HALF, 2], F32) for m in PAIRED_TILES + (DIRECT_TILE,) for hf in range(2)
+        }
+        sums = sb("sums", [P, S], F32)
+        total = sb("total", [P, S], F32)
+        logs = sb("logs", [P, ROW_TILES, S], F32, after="pairs%d_1" % PAIRED_TILES[-1])
+        res = [sb("res%d" % m, [P, S], F32) for m in range(ROW_TILES)]
+        turned = {m: bank("turned%d" % m, S, m + PACK) for m in TURNED_TILES}
+        back = {m: bank("back%d" % m, S, m) for m in TURNED_TILES}
 
-        def gather_members(engine, m, a, b):
-            src = ex[m][:].indirect(cols(n3_t, a * MEMBERS, b * MEMBERS))
-            dst = members[m][:, a:b, :].rearrange("p j t -> p (j t)")
+        def gather_members(engine, m, first, last):
+            src = ex[m][:].indirect(entries(n3_t, first * MEMBERS, last * MEMBERS))
+            dst = members[m][:, first:last, :].rearrange("p s t -> p (s t)")
             if engine == "vector":
                 nc.vector.tensor_copy(out=dst, in_=src)
             else:
                 nc.scalar.activation(out=dst, in_=src, func=ACT.Copy)
 
-        def add_turned(m, blk):
-            js = slice(blk * P, (blk + 1) * P)
-            terms = [members[m][:, js, t] for t in range(MEMBERS)] + [ex[m][:, js]]
-            for i, term in enumerate(terms):
-                nc.tensor.matmul(out=turned[m][:, js], lhsT=term, rhs=ident[:], is_transpose=True, start=(i == 0), stop=(i == MEMBERS))
-
-        def log_turned(m):
-            nc.scalar.activation(out=logs[m][:], in_=turned[m][:], func=ACT.Ln)
-            for blk in range(S // P):
-                js = slice(blk * P, (blk + 1) * P)
-                nc.tensor.transpose(back[m][:, js], logs[m][:, js], ident[:])
-
-        def finish_turned(m):
-            nc.vector.tensor_tensor(out=res[m][:], in0=back[m][:], in1=h_sb[m][:], op=ALU.subtract)
-            nc.sync.dma_start(out=out[m * P : (m + 1) * P, :], in_=res[m][:])
-
-        def add_members(engine, m, halves):
-            for hf in halves:
-                js = slice(hf * HALF, (hf + 1) * HALF)
-                engine.tensor_tensor(out=pairs[m, hf][:], in0=members[m][:, js, 0:2], in1=members[m][:, js, 2:4], op=ALU.add)
-            for hf in halves:
-                js = slice(hf * HALF, (hf + 1) * HALF)
-                engine.tensor_tensor(out=sums[m][:, js], in0=pairs[m, hf][:, :, 0], in1=pairs[m, hf][:, :, 1], op=ALU.add)
-            for hf in halves:
-                js = slice(hf * HALF, (hf + 1) * HALF)
-                engine.tensor_tensor(out=total[m][:, js], in0=sums[m][:, js], in1=ex[m][:, js], op=ALU.add)
-
-        def take_log(m, a, b):
-            nc.scalar.activation(out=logs[m][:, a:b], in_=total[m][:, a:b], func=ACT.Ln)
-
-        def finish(m, a, b):
-            hf = a // HALF
-            nc.vector.tensor_tensor(
-                out=res[m][:, a:b], in0=logs[m][:, a:b], in1=h_ps[m][hf][:, a - hf * HALF : b - hf * HALF], op=ALU.subtract
+        def add_pairs(engine, m, hf):
+            engine.tensor_tensor(
+                out=pairs[m, hf][:], in0=members[m][:, half(hf), 0:2], in1=members[m][:, half(hf), 2:4], op=ALU.add
             )
-            nc.sync.dma_start(out=out[m * P : (m + 1) * P, a:b], in_=res[m][:, a:b])
 
-        for m, hf in ((0, 0), (2, 0), (0, 1), (2, 1), (1, 0), (1, 1), (3, 0), (3, 1)):
+        def add_turned(m, blk):
+            if m in PAIRED_TILES:
+                terms = [pairs[m, blk // 2][:, block(blk % 2), t] for t in range(2)]
+            else:
+                terms = [members[m][:, block(blk), t] for t in range(MEMBERS)]
+            terms = terms + [ex[m][:, block(blk)]]
+            for i, term in enumerate(terms):
+                nc.tensor.matmul(
+                    out=turned[m][:, block(blk)], lhsT=term, rhs=ident[:],
+                    is_transpose=True, start=(i == 0), stop=(i == len(terms) - 1),
+                )
+
+        order = [(m, hf) for hf in range(2) for m in range(2)] + [(m, hf) for m in range(2, ROW_TILES) for hf in range(2)]
+        for m, hf in order:
             for engine, blk in (("vector", 2 * hf), ("scalar", 2 * hf + 1)):
-                a, b = blk * P, (blk + 1) * P
-                if (m, blk) == (3, 3):
-                    gather_members("vector", m, a, a + 32)
-                    a = a + 32
-                gather_members(engine, m, a, b)
-                if m in TENSOR_TILES:
-                    add_turned(m, blk)
-            if (m, hf) == (1, 1):
+                first, last = blk * P, (blk + 1) * P
+                if m == DIRECT_TILE and last == S:
+                    gather_members("vector", m, first, first + LAST_SHARE)
+                    first = first + LAST_SHARE
+                gather_members(engine, m, first, last)
+            if m in PAIRED_TILES:
+                add_pairs(nc.gpsimd, m, hf)
+            if m in TURNED_TILES:
+                add_turned(m, 2 * hf)
+                add_turned(m, 2 * hf + 1)
+            if (m, hf) == (TURNED_TILES[-1], 1):
                 copy_h(1)
-        add_members(nc.gpsimd, 2, [0])
-        add_members(nc.gpsimd, 2, [1])
-        add_members(nc.vector, 3, [0, 1])
-        for m in (0, 2, 1, 3):
-            if m in TENSOR_TILES:
-                log_turned(m)
-            else:
-                take_log(m, 0, S)
-        for m in (2, 0, 1, 3):
-            if m in TENSOR_TILES:
-                finish_turned(m)
-            else:
-                for hf in range(2):
-                    finish(m, hf * HALF, (hf + 1) * HALF)
+
+        for hf in range(2):
+            add_pairs(nc.vector, DIRECT_TILE, hf)
+        for hf in range(2):
+            two_sums = pairs[DIRECT_TILE, hf]
+            nc.vector.tensor_tensor(out=sums[:, half(hf)], in0=two_sums[:, :, 0], in1=two_sums[:, :, 1], op=ALU.add)
+        for hf in range(2):
+            nc.vector.tensor_tensor(out=total[:, half(hf)], in0=sums[:, half(hf)], in1=ex[DIRECT_TILE][:, half(hf)], op=ALU.add)
+
+        for m in TURNED_TILES:
+            nc.scalar.activation(out=logs[:, m, :], in_=turned[m][:], func=ACT.Ln)
+            for blk in range(S // P):
+                nc.tensor.transpose(back[m][:, block(blk)], logs[:, m, block(blk)], ident[:])
+        nc.scalar.activation(out=logs[:, DIRECT_TILE, :], in_=total[:], func=ACT.Ln)
+
+        for m in TURNED_TILES:
+            nc.vector.tensor_tensor(out=res[m][:], in0=back[m][:], in1=h_sb[:, m, :], op=ALU.subtract)
+            nc.sync.dma_start(out=out[block(m), :], in_=res[m][:])
+        for hf in range(2):
+            dst = res[DIRECT_TILE][:, half(hf)]
+            nc.vector.tensor_tensor(out=dst, in0=logs[:, DIRECT_TILE, half(hf)], in1=h_ps[DIRECT_TILE][hf][:], op=ALU.subtract)
+            nc.sync.dma_start(out=out[block(DIRECT_TILE), half(hf)], in_=dst)

from contextlib import ExitStack

import concourse.mybir as mybir
from concourse.masks import make_identity

K, T, S, N, H, W = 512, 2048, 512, 512, 512, 2048
FLOPS = 2 * S * (K * H + H * N + K * N)

F32 = mybir.dt.float32
BF16 = mybir.dt.bfloat16
I32 = mybir.dt.int32
U32 = mybir.dt.uint32
U16 = mybir.dt.uint16
U8 = mybir.dt.uint8
FP8X4 = mybir.dt.float8_e4m3fn_x4
ACT = mybir.ActivationFunctionType
ALU = mybir.AluOpType

P = 128
PACK = 4
STRIPE = 16
LINE = 4
HALF = S // 2
MEMBERS = W // S
ROW_TILES = N // P
SPARE = 32
Y_ON_VECTOR = 1
N2_ON_VECTOR = (0, 0)
TURNED_TILES = (0, 1, 2)
PAIRED_TILES = (1, 2)
DIRECT_TILE = 3
LAST_SHARE = 32


def half(hf):
    return slice(hf * HALF, (hf + 1) * HALF)


def block(blk):
    return slice(blk * P, (blk + 1) * P)


def entries(list_tile, first, last):
    return list_tile[:, first // STRIPE : last // STRIPE]


def tile_picked_mixingmaxglse_none_p_kernel(
    tc, x_words, x_scales, w1, gn, w2, w3, offs, n1, n2, two, n3, out
):
    nc = tc.nc
    with ExitStack() as ctx:
        keep = ctx.enter_context(tc.tile_pool(name="keep", bufs=1))
        psum = ctx.enter_context(tc.psum_pool(name="psum", bufs=1))

        def sb(name, shape, dtype, after=None):
            return keep.tile(shape, dtype, name=name, tag=after or name, align_bytes=64)

        def bank(name, width, number):
            return psum.tile([P, width], F32, name=name, tag="bank%d" % number)

        def quantize(codes, scales, values):
            nc.vector.quantize_mx(out=codes.bitcast(FP8X4), scales=scales, in_=values)

        def product(dst, w_codes, w_scales, x_codes, x_bytes, start, stop):
            nc.tensor.matmul_mx(
                out=dst,
                lhsT=w_codes.bitcast(FP8X4),
                lhsT_scale=w_scales,
                rhs=x_codes.bitcast(FP8X4),
                rhs_scale=x_bytes,
                start=start,
                stop=stop,
            )

        offs_t = sb("offs_t", [P, S // STRIPE], U16)
        two_t = sb("two_t", [P, S // STRIPE], U16)
        n1_t = sb("n1_t", [P, S // STRIPE], U16)
        n2_t = sb("n2_t", [P, S // STRIPE], U16)
        n3_t = sb("n3_t", [P, W // STRIPE], U16)
        words = sb("words", [P, T], U32)
        scale_bytes = sb("scale_bytes", [P, T], U8)
        w1_raw = sb("w1_raw", [P, PACK, H], F32)
        w2_raw = sb("w2_raw", [P, PACK, N], F32)
        w3_raw = sb("w3_raw", [P, PACK, N], F32)
        gain = sb("gain", [P, PACK], F32)
        ex = [sb("ex%d" % m, [P, S + SPARE], F32) for m in range(ROW_TILES)]

        nc.gpsimd.memset(scale_bytes[:].bitcast(I32), 0)
        for m in range(ROW_TILES):
            nc.gpsimd.memset(ex[m][:, S:], 0.0)
        ident = sb("ident", [P, P], F32)
        make_identity(nc, ident[:])

        warm = sb("warm", [P, 1], F32)
        nc.scalar.activation(out=warm[:], in_=ex[0][:, S : S + 1], func=ACT.Sigmoid)

        nc.sync.dma_start(offs_t[:], offs)
        nc.sync.dma_start(two_t[:], two)
        for q in range(4):
            nc.sync.dma_start(
                out=scale_bytes[32 * q : 32 * q + 4, :].bitcast(I32),
                in_=x_scales[0, 4 * q : 4 * q + 4, :].bitcast(I32),
            )
        nc.sync.dma_start(out=w1_raw[:], in_=w1.rearrange("(p j) c -> p j c", j=PACK))
        nc.sync.dma_start(out=words[:].bitcast(I32), in_=x_words[0].rearrange("p n j -> p (n j)").bitcast(I32))
        nc.sync.dma_start(n1_t[:], n1)
        nc.sync.dma_start(n2_t[:], n2)
        nc.sync.dma_start(out=w3_raw[:], in_=w3.rearrange("(p j) c -> p j c", j=PACK))
        nc.sync.dma_start(out=gain[:], in_=gn.rearrange("(p t) o -> p (t o)", t=PACK))
        nc.sync.dma_start(out=w2_raw[:], in_=w2.rearrange("(p j) c -> p j c", j=PACK))
        nc.sync.dma_start(n3_t[:], n3)

        w1_codes = [sb("w1_codes%d" % u, [P, 2 * P], U32) for u in range(2)]
        w1_scales = [sb("w1_scales%d" % u, [P, 2 * P], U8) for u in range(2)]
        w1_bf = [sb("w1_bf%d" % u, [P, 2, P, PACK], BF16) for u in range(2)]
        xa_bytes = sb("xa_bytes", [P, S], U8)
        xb_bytes = sb("xb_bytes", [P, S], U8)
        xa_words = [sb("xa_words%d" % hf, [P, HALF], U32) for hf in range(2)]
        xb_words = sb("xb_words", [P, S], U32)
        nc.vector.tensor_copy(out=xa_bytes[:], in_=scale_bytes[:].indirect(offs_t[:]))
        nc.vector.tensor_copy(out=xb_bytes[:], in_=scale_bytes[:].indirect(two_t[:]))

        for u, cast in enumerate((nc.scalar.copy, nc.vector.tensor_copy)):
            cast(
                out=w1_bf[u][:].rearrange("p t c j -> p c j t"),
                in_=w1_raw[:].rearrange("p j (c t) -> p c j t", t=PACK)[:, :, :, 2 * u : 2 * u + 2],
            )
        for u in range(2):
            quantize(w1_codes[u][:], w1_scales[u][:], w1_bf[u][:].rearrange("p t c j -> p (t c j)"))
        for hf in range(2):
            nc.vector.tensor_copy(out=xa_words[hf][:], in_=words[:].indirect(entries(offs_t, hf * HALF, (hf + 1) * HALF)))
        nc.vector.tensor_copy(out=xb_words[:], in_=words[:].indirect(two_t[:]))

        y_ps = [bank("y_ps%d" % t, S, t) for t in range(PACK)]
        for u in range(2):
            for hf in range(2):
                for t in (2 * u, 2 * u + 1):
                    cs = block(t % 2)
                    product(
                        y_ps[t][:, half(hf)], w1_codes[u][:, cs], w1_scales[u][:, cs],
                        xa_words[hf][:], xa_bytes[:, half(hf)], True, True,
                    )

        y = [sb("y%d" % t, [P, S], F32) for t in range(PACK)]
        gate = [sb("gate%d" % hf, [P, PACK, HALF], F32) for hf in range(2)]
        other = [sb("other%d" % hf, [P, PACK, HALF], F32) for hf in range(2)]
        larger = [sb("larger%d" % hf, [P, PACK, HALF], F32) for hf in range(2)]
        z_bf = [sb("z_bf%d" % hf, [P, HALF, PACK], BF16) for hf in range(2)]
        z_codes = [sb("z_codes%d" % hf, [P, HALF], U32) for hf in range(2)]
        z_scales = [sb("z_scales%d" % hf, [P, HALF], U8) for hf in range(2)]

        def copy_y(t):
            if t == Y_ON_VECTOR:
                nc.vector.tensor_copy(out=y[t][:], in_=y_ps[t][:])
            else:
                nc.scalar.copy(out=y[t][:], in_=y_ps[t][:])

        def gather_gate(hf, t):
            src = y[t][:].indirect(entries(n1_t, hf * HALF, (hf + 1) * HALF))
            nc.scalar.activation(out=gate[hf][:, t, :], in_=src, func=ACT.Sigmoid)

        def gather_other(hf, t):
            src = y[t][:].indirect(entries(n2_t, hf * HALF, (hf + 1) * HALF))
            if (hf, t) == N2_ON_VECTOR:
                nc.vector.tensor_copy(out=other[hf][:, t, :], in_=src)
            else:
                nc.scalar.activation(out=other[hf][:, t, :], in_=src, func=ACT.Copy)

        def apply_gate(hf, t):
            dst = gated[2 * hf + t // 2][:, t % 2, :]
            nc.vector.tensor_tensor(out=dst, in0=gate[hf][:, t, :], in1=y[t][:, half(hf)], op=ALU.mult)

        def take_larger(hf, t):
            src = gated[2 * hf + t // 2][:, t % 2, :]
            nc.vector.tensor_tensor(out=larger[hf][:, t, :], in0=src, in1=other[hf][:, t, :], op=ALU.max)

        def make_z(hf):
            nc.vector.tensor_tensor(
                out=z_bf[hf][:].rearrange("p (g i) t -> p g t i", i=LINE),
                in0=larger[hf][:].rearrange("p t (g i) -> p g t i", i=LINE),
                in1=gain[:].unsqueeze(1).unsqueeze(3).to_broadcast([P, HALF // LINE, PACK, LINE]),
                op=ALU.mult,
            )
            quantize(z_codes[hf][:], z_scales[hf][:], z_bf[hf][:].rearrange("p s t -> p (s t)"))

        def round_weight(name, raw):
            bf = sb(name + "_bf", [P, N, PACK], BF16)
            codes = sb(name + "_codes", [P, N], U32)
            scales = sb(name + "_scales", [P, N], U8)
            nc.vector.tensor_copy(
                out=bf[:].rearrange("p (g i) j -> p g j i", i=LINE),
                in_=raw[:].rearrange("p j (g i) -> p g j i", i=LINE),
            )
            return bf, codes, scales

        copy_y(Y_ON_VECTOR)
        w3_bf, w3_codes, w3_scales = round_weight("w3", w3_raw)
        w2_bf, w2_codes, w2_scales = round_weight("w2", w2_raw)
        quantize(w3_codes[:], w3_scales[:], w3_bf[:].rearrange("p n j -> p (n j)"))
        quantize(w2_codes[:], w2_scales[:], w2_bf[:].rearrange("p n j -> p (n j)"))
        taken_over = ("w3_raw", "w2_raw", "w2_raw", "larger0")
        gated = [sb("gated%d" % i, [P, 2, HALF], F32, after=name) for i, name in enumerate(taken_over)]
        for t in range(PACK):
            if t != Y_ON_VECTOR:
                copy_y(t)
            gather_gate(0, t)
            gather_other(0, t)
            apply_gate(0, t)
            take_larger(0, t)
        make_z(0)
        for t in range(PACK):
            gather_gate(1, t)
            apply_gate(1, t)
        for t in range(PACK):
            gather_other(1, t)
            take_larger(1, t)
        make_z(1)

        h_ps = [[bank("h_ps%d_%d" % (m, hf), HALF, m + PACK * (1 - hf)) for hf in range(2)] for m in range(ROW_TILES)]
        for hf in range(2):
            for m in range(ROW_TILES):
                product(
                    h_ps[m][hf][:], w3_codes[:, block(m)], w3_scales[:, block(m)],
                    xb_words[:, half(hf)], xb_bytes[:, half(hf)], True, False,
                )
        for hf in range(2):
            for m in range(ROW_TILES):
                product(
                    h_ps[m][hf][:], w2_codes[:, block(m)], w2_scales[:, block(m)],
                    z_codes[hf][:], z_scales[hf][:], False, True,
                )

        h_sb = sb("h_sb", [P, len(TURNED_TILES), S], F32, after="z_bf1")

        def copy_h(hf):
            for m in TURNED_TILES:
                nc.vector.tensor_copy(out=h_sb[:, m, half(hf)], in_=h_ps[m][hf][:])

        for hf in range(2):
            for m in range(ROW_TILES):
                nc.scalar.activation(out=ex[m][:, half(hf)], in_=h_ps[m][hf][:], func=ACT.Exp)
            if hf == 0:
                copy_h(0)

        members = [sb("members%d" % m, [P, S, MEMBERS], F32) for m in range(ROW_TILES)]
        pairs = {
            (m, hf): sb("pairs%d_%d" % (m, hf), [P, HALF, 2], F32) for m in PAIRED_TILES + (DIRECT_TILE,) for hf in range(2)
        }
        sums = sb("sums", [P, S], F32)
        total = sb("total", [P, S], F32)
        logs = sb("logs", [P, ROW_TILES, S], F32, after="pairs%d_1" % PAIRED_TILES[-1])
        res = [sb("res%d" % m, [P, S], F32) for m in range(ROW_TILES)]
        turned = {m: bank("turned%d" % m, S, m + PACK) for m in TURNED_TILES}
        back = {m: bank("back%d" % m, S, m) for m in TURNED_TILES}

        def gather_members(engine, m, first, last):
            src = ex[m][:].indirect(entries(n3_t, first * MEMBERS, last * MEMBERS))
            dst = members[m][:, first:last, :].rearrange("p s t -> p (s t)")
            if engine == "vector":
                nc.vector.tensor_copy(out=dst, in_=src)
            else:
                nc.scalar.activation(out=dst, in_=src, func=ACT.Copy)

        def add_pairs(engine, m, hf):
            engine.tensor_tensor(
                out=pairs[m, hf][:], in0=members[m][:, half(hf), 0:2], in1=members[m][:, half(hf), 2:4], op=ALU.add
            )

        def add_turned(m, blk):
            if m in PAIRED_TILES:
                terms = [pairs[m, blk // 2][:, block(blk % 2), t] for t in range(2)]
            else:
                terms = [members[m][:, block(blk), t] for t in range(MEMBERS)]
            terms = terms + [ex[m][:, block(blk)]]
            for i, term in enumerate(terms):
                nc.tensor.matmul(
                    out=turned[m][:, block(blk)], lhsT=term, rhs=ident[:],
                    is_transpose=True, start=(i == 0), stop=(i == len(terms) - 1),
                )

        order = [(m, hf) for hf in range(2) for m in range(2)] + [(m, hf) for m in range(2, ROW_TILES) for hf in range(2)]
        for m, hf in order:
            for engine, blk in (("vector", 2 * hf), ("scalar", 2 * hf + 1)):
                first, last = blk * P, (blk + 1) * P
                if m == DIRECT_TILE and last == S:
                    gather_members("vector", m, first, first + LAST_SHARE)
                    first = first + LAST_SHARE
                gather_members(engine, m, first, last)
            if m in PAIRED_TILES:
                add_pairs(nc.gpsimd, m, hf)
            if m in TURNED_TILES:
                add_turned(m, 2 * hf)
                add_turned(m, 2 * hf + 1)
            if (m, hf) == (TURNED_TILES[-1], 1):
                copy_h(1)

        for hf in range(2):
            add_pairs(nc.vector, DIRECT_TILE, hf)
        for hf in range(2):
            two_sums = pairs[DIRECT_TILE, hf]
            nc.vector.tensor_tensor(out=sums[:, half(hf)], in0=two_sums[:, :, 0], in1=two_sums[:, :, 1], op=ALU.add)
        for hf in range(2):
            nc.vector.tensor_tensor(out=total[:, half(hf)], in0=sums[:, half(hf)], in1=ex[DIRECT_TILE][:, half(hf)], op=ALU.add)

        for m in TURNED_TILES:
            nc.scalar.activation(out=logs[:, m, :], in_=turned[m][:], func=ACT.Ln)
            for blk in range(S // P):
                nc.tensor.transpose(back[m][:, block(blk)], logs[:, m, block(blk)], ident[:])
        nc.scalar.activation(out=logs[:, DIRECT_TILE, :], in_=total[:], func=ACT.Ln)

        for m in TURNED_TILES:
            nc.vector.tensor_tensor(out=res[m][:], in0=back[m][:], in1=h_sb[:, m, :], op=ALU.subtract)
            nc.sync.dma_start(out=out[block(m), :], in_=res[m][:])
        for hf in range(2):
            dst = res[DIRECT_TILE][:, half(hf)]
            nc.vector.tensor_tensor(out=dst, in0=logs[:, DIRECT_TILE, half(hf)], in1=h_ps[DIRECT_TILE][hf][:], op=ALU.subtract)
            nc.sync.dma_start(out=out[block(DIRECT_TILE), half(hf)], in_=dst)
